import numpy as np
import ml_dtypes


def mxq(x, axis, fmt="e4m3"):
    dtype, down = {"e4m3": (ml_dtypes.float8_e4m3fn, 7), "e5m2": (ml_dtypes.float8_e5m2, 14)}[fmt]
    v = np.moveaxis(np.asarray(x, np.float32).astype(ml_dtypes.bfloat16).astype(np.float64), axis, -1)
    blocks = v.reshape(v.shape[:-1] + (-1, 32))
    amax = np.abs(blocks).max(-1, keepdims=True)
    byte = np.maximum(np.where(amax > 0, np.frexp(amax)[1] - 1 + 127, 0) - down, 1)
    scale = np.exp2(byte - 127.0)
    codes = (blocks / scale).astype(np.float32).astype(dtype).astype(np.float64)
    return np.moveaxis((codes * scale).reshape(v.shape), -1, axis)


WIDE = False


def mx_kscale(k):
    if not WIDE:
        return np.ones(k)
    levels = np.array([10, -10, 5, -5, 0])
    if k % 512:
        return np.exp2(np.random.permutation(np.resize(levels, k // 32))).repeat(32)
    a = np.empty((k // 512, 16))
    for p in range(k // 512):
        a[p, :8] = np.random.permutation(np.resize(levels, 8))
        for g in range(8):
            far = levels[np.abs(levels - a[p, g]) >= 10]
            a[p, g + 8] = far[np.random.randint(len(far))]
    return np.exp2(a.ravel()).repeat(32)


def f64(x):
    return np.asarray(x).astype(np.float64)


def striped(idx):
    return np.tile(np.asarray(idx).reshape(-1, 16).T, (8, 1)).astype(np.uint16)


def unstriped(offs):
    return offs[:16].T.reshape(-1).astype(np.int64)


E, T, I, J, F = 512, 2048, 512, 512, 512


def setup_inputs():
    n = np.random.standard_normal
    idx = np.random.permutation(T)[:I]
    fe = mx_kscale(E)
    fi = mx_kscale(I)
    ti = np.ones(T)
    ti[idx] = fi
    return {
        "tok": (n((E, T)) / fe[:, None] / ti).astype(np.float32),
        "ci": ((np.cos(2 * np.pi * np.arange(I)[:, None] * np.arange(J) / I) / np.sqrt(I)) * fi[:, None]).astype(np.float32),
        "si": ((np.sin(2 * np.pi * np.arange(I)[:, None] * np.arange(J) / I) / np.sqrt(I)) * fi[:, None]).astype(np.float32),
        "ce": ((2.0 * np.cos(2 * np.pi * np.arange(E)[:, None] * np.arange(F) / E) / np.sqrt(E)) * fe[:, None]).astype(np.float32),
        "se": ((-2.0 * np.sin(2 * np.pi * np.arange(E)[:, None] * np.arange(F) / E) / np.sqrt(E)) * fe[:, None]).astype(np.float32),
        "offs": striped(idx),
    }


def reference(tok, ci, si, ce, se, offs):
    idx = unstriped(offs)
    xt = f64(tok)[:, idx].T
    ciq = mxq(f64(ci), 0, "e4m3")
    xtq = mxq(xt, 0, "e4m3")
    a = ciq.T @ xtq
    siq = mxq(f64(si), 0, "e4m3")
    b = siq.T @ xtq
    at = a.T
    bt = b.T
    ceq = mxq(f64(ce), 0, "e4m3")
    atq = mxq(at, 0, "e4m3")
    seq = mxq(f64(se), 0, "e4m3")
    btq = mxq(bt, 0, "e4m3")
    y = ceq.T @ atq + seq.T @ btq
    return y

@@ -1,0 +1,169 @@
+from contextlib import ExitStack
+
+import concourse.mybir as mybir
+from concourse.masks import make_identity
+
+E, T, I, J, F = 512, 2048, 512, 512, 512
+FLOPS = 2 * (2 * I * J * E + 2 * E * F * J)
+
+F32 = mybir.dt.float32
+BF16 = mybir.dt.bfloat16
+U32 = mybir.dt.uint32
+U16 = mybir.dt.uint16
+U8 = mybir.dt.uint8
+FP8X4 = mybir.dt.float8_e4m3fn_x4
+
+P = 128
+PACK = 4
+LINE = 4
+
+
+def tile_attend_fouriermix_kernel(tc, tok, ci, si, ce, se, offs, out):
+    nc = tc.nc
+    with ExitStack() as ctx:
+        sb = ctx.enter_context(tc.tile_pool(name="sb", bufs=1))
+        ps = ctx.enter_context(tc.psum_pool(name="ps", bufs=1))
+
+        def bank(n, shape, name):
+            return ps.tile(shape, F32, name=name, tag="bank%d" % n)
+
+        def mx_tiles(width, name):
+            codes = sb.tile([P, width], U32, name=name + "_codes", align_bytes=64)
+            scales = sb.tile([P, width], U8, name=name + "_scales", align_bytes=64)
+            return codes, scales
+
+        def quantise(dst, c0, grouped):
+            width = grouped.shape[1]
+            nc.vector.quantize_mx(
+                out=dst[0][:, c0 : c0 + width].bitcast(FP8X4),
+                scales=dst[1][:, c0 : c0 + width],
+                in_=grouped[:].rearrange("p w t -> p (w t)"),
+            )
+
+        def copy(engine, dst, src):
+            if engine == "v":
+                nc.vector.tensor_copy(out=dst, in_=src)
+            else:
+                nc.scalar.copy(out=dst, in_=src)
+
+        def load(matrix, c0, width, name):
+            raw = sb.tile([P, PACK, width], F32, name=name + "_raw")
+            nc.sync.dma_start(out=raw[:], in_=matrix[:, c0 : c0 + width].rearrange("(p t) w -> p t w", t=PACK))
+            return raw
+
+        def weave(engine, raw, c0, width, name):
+            grouped = sb.tile([P, width, PACK], BF16, name=name + "_grouped", align_bytes=64)
+            copy(
+                engine,
+                grouped[:].rearrange("p (c i) t -> p c t i", i=LINE),
+                raw[:, :, c0 : c0 + width].rearrange("p t (c i) -> p c t i", i=LINE),
+            )
+            return grouped
+
+        def mm(dst, lhs, l0, rhs, r0, n, start, stop):
+            nc.tensor.matmul_mx(
+                out=dst,
+                lhsT=lhs[0][:, l0 : l0 + P].bitcast(FP8X4),
+                lhsT_scale=lhs[1][:, l0 : l0 + P],
+                rhs=rhs[0][:, r0 : r0 + n].bitcast(FP8X4),
+                rhs_scale=rhs[1][:, r0 : r0 + n],
+                start=start,
+                stop=stop,
+            )
+
+        identity = sb.tile([P, P], F32, name="identity")
+        make_identity(nc, identity[:])
+
+        offsets = sb.tile([P, I // 16], U16, name="offsets")
+        planes = [sb.tile([P, T], F32, name="plane%d" % t) for t in range(PACK)]
+        tok_planes = tok.rearrange("(p t) n -> t p n", t=PACK)
+        nc.sync.dma_start(out=planes[0][:], in_=tok_planes[0])
+        nc.sync.dma_start(offsets[:], offs)
+        for t in range(1, PACK):
+            nc.sync.dma_start(out=planes[t][:], in_=tok_planes[t])
+        H = 256
+        ci_raw = [load(ci, h * H, H, "ci%d" % h) for h in range(2)]
+        si_raw = [load(si, h * H, H, "si%d" % h) for h in range(2)]
+        ce0_raw = load(ce, 0, H, "ce0")
+        se0_raw = load(se, 0, H, "se0")
+        ce1_raw = load(ce, H, H, "ce1")
+        se1_raw = load(se, H, H, "se1")
+
+        xq = [mx_tiles(P, "xq%d" % t) for t in range(PACK)]
+
+        def tokens(t, engine):
+            picked = sb.tile([P, I], BF16, name="picked%d" % t, align_bytes=64)
+            nc.vector.tensor_copy(picked[:], planes[t][:].indirect(offsets[:]))
+            words = picked[:].bitcast(F32)
+            turned = bank(4 + t, [P, 2, P], "turned%d" % t)
+            for u in range(2):
+                nc.tensor.transpose(turned[:, u, :], words[:, u : I // 2 : 2], identity[:])
+            grouped = sb.tile([P, P, PACK], BF16, name="xt%d_grouped" % t, align_bytes=64)
+            copy(
+                engine,
+                grouped[:].rearrange("p w t -> p (w t)").bitcast(F32).rearrange("p (w u) -> p w u", u=2),
+                turned[:].rearrange("p u w -> p w u"),
+            )
+            return grouped
+
+        def stage1(first_bank, q, c0, dst, d0, name, engine):
+            acc = bank(first_bank, [P, PACK, P], name)
+            for t in range(PACK):
+                mm(acc[:, t, :], xq[t], 0, q, c0, P, True, True)
+            copy(engine, dst[:, d0 : d0 + P, :], acc[:].rearrange("p t j -> p j t"))
+
+        for t in range(PACK - 1):
+            quantise(xq[t], 0, tokens(t, "s"))
+        last_tokens = tokens(PACK - 1, "s")
+
+        ciq = [mx_tiles(H, "ciq%d" % h) for h in range(2)]
+        siq = [mx_tiles(H, "siq%d" % h) for h in range(2)]
+        ceq = [mx_tiles(H, "ceq%d" % h) for h in range(2)]
+        seq = [mx_tiles(H, "seq%d" % h) for h in range(2)]
+        aq = mx_tiles(J, "aq")
+        bq = mx_tiles(J, "bq")
+        ag = [sb.tile([P, H, PACK], BF16, name="ag%d" % h, align_bytes=64) for h in range(2)]
+        bg = [sb.tile([P, H, PACK], BF16, name="bg%d" % h, align_bytes=64) for h in range(2)]
+
+        def half_stage1(first_bank, q, dst, name):
+            for c in range(2):
+                stage1(first_bank + c, q, c * P, dst, c * P, "%s%d" % (name, c), "s")
+
+        def finish(c, parts):
+            result = sb.tile([P, J], F32, name="result%d" % c)
+            for n, engine, j0, width in parts:
+                acc = bank(n, [P, width], "y%d_%d" % (c, j0))
+                mm(acc[:], ceq[c // 2], (c % 2) * P, aq, j0, width, True, False)
+                mm(acc[:], seq[c // 2], (c % 2) * P, bq, j0, width, False, True)
+                copy(engine, result[:, j0 : j0 + width], acc[:])
+            nc.sync.dma_start(out=out[c * P : (c + 1) * P, :], in_=result[:])
+
+        ci0 = weave("v", ci_raw[0], 0, H, "ci0")
+        quantise(xq[PACK - 1], 0, last_tokens)
+        quantise(ciq[0], 0, ci0)
+        ci1 = weave("s", ci_raw[1], 0, H, "ci1")
+        half_stage1(0, ciq[0], ag[0], "a0")
+        si0 = weave("v", si_raw[0], 0, H, "si0")
+        quantise(ciq[1], 0, ci1)
+        quantise(siq[0], 0, si0)
+        half_stage1(2, ciq[1], ag[1], "a1")
+        half_stage1(4, siq[0], bg[0], "b0")
+        si1 = weave("v", si_raw[1], 0, H, "si1")
+        quantise(aq, 0, ag[0])
+        quantise(siq[1], 0, si1)
+        half_stage1(6, siq[1], bg[1], "b1")
+        ce0 = weave("v", ce0_raw, 0, H, "ce0")
+        quantise(aq, H, ag[1])
+        quantise(ceq[0], 0, ce0)
+        se0 = weave("v", se0_raw, 0, H, "se0")
+        quantise(bq, 0, bg[0])
+        quantise(seq[0], 0, se0)
+        ce1 = weave("s", ce1_raw, 0, H, "ce1")
+        quantise(bq, H, bg[1])
+        finish(0, [(0, "s", 0, J)])
+        se1 = weave("v", se1_raw, 0, H, "se1")
+        quantise(ceq[1], 0, ce1)
+        quantise(seq[1], 0, se1)
+        finish(1, [(1, "s", 0, J)])
+        finish(2, [(2, "v", 0, J)])
+        finish(3, [(4, "s", 0, H), (5, "v", H, H)])

@@ -15,7 +15,7 @@ FP8X4 = mybir.dt.float8_e4m3fn_x4
 
 P = 128
 PACK = 4
-LINE = 4
+LINE = 2
 
 
 def tile_attend_fouriermix_kernel(tc, tok, ci, si, ce, se, offs, out):
@@ -27,8 +27,8 @@ def tile_attend_fouriermix_kernel(tc, tok, ci, si, ce, se, offs, out):
         def bank(n, shape, name):
             return ps.tile(shape, F32, name=name, tag="bank%d" % n)
 
-        def mx_tiles(width, name):
-            codes = sb.tile([P, width], U32, name=name + "_codes", align_bytes=64)
+        def mx_tiles(width, name, tag=None):
+            codes = sb.tile([P, width], U32, name=name + "_codes", tag=tag or name + "_codes", align_bytes=64)
             scales = sb.tile([P, width], U8, name=name + "_scales", align_bytes=64)
             return codes, scales
 
@@ -47,12 +47,12 @@ def tile_attend_fouriermix_kernel(tc, tok, ci, si, ce, se, offs, out):
                 nc.scalar.copy(out=dst, in_=src)
 
         def load(matrix, c0, width, name):
-            raw = sb.tile([P, PACK, width], F32, name=name + "_raw")
+            raw = sb.tile([P, PACK, width], F32, name=name + "_raw", tag=name + "_raw", align_bytes=64)
             nc.sync.dma_start(out=raw[:], in_=matrix[:, c0 : c0 + width].rearrange("(p t) w -> p t w", t=PACK))
             return raw
 
         def weave(engine, raw, c0, width, name):
-            grouped = sb.tile([P, width, PACK], BF16, name=name + "_grouped", align_bytes=64)
+            grouped = sb.tile([P, width, PACK], BF16, name=name + "_grouped", tag=name + "_grouped", align_bytes=64)
             copy(
                 engine,
                 grouped[:].rearrange("p (c i) t -> p c t i", i=LINE),
@@ -82,14 +82,17 @@ def tile_attend_fouriermix_kernel(tc, tok, ci, si, ce, se, offs, out):
         for t in range(1, PACK):
             nc.sync.dma_start(out=planes[t][:], in_=tok_planes[t])
         H = 256
-        ci_raw = [load(ci, h * H, H, "ci%d" % h) for h in range(2)]
-        si_raw = [load(si, h * H, H, "si%d" % h) for h in range(2)]
+        ci0_raw = load(ci, 0, H, "ci0")
+        si0_raw = load(si, 0, H, "si0")
+        ci1_raw = load(ci, H, H, "ci1")
+        si1_raw = load(si, H, H, "si1")
         ce0_raw = load(ce, 0, H, "ce0")
         se0_raw = load(se, 0, H, "se0")
         ce1_raw = load(ce, H, H, "ce1")
         se1_raw = load(se, H, H, "se1")
 
-        xq = [mx_tiles(P, "xq%d" % t) for t in range(PACK)]
+        xq = [mx_tiles(2 * P, "xq0")]
+        xg = [sb.tile([P, 2 * P, PACK], BF16, name="xg%d" % g, align_bytes=64) for g in range(2)]
 
         def tokens(t, engine):
             picked = sb.tile([P, I], BF16, name="picked%d" % t, align_bytes=64)
@@ -98,72 +101,112 @@ def tile_attend_fouriermix_kernel(tc, tok, ci, si, ce, se, offs, out):
             turned = bank(4 + t, [P, 2, P], "turned%d" % t)
             for u in range(2):
                 nc.tensor.transpose(turned[:, u, :], words[:, u : I // 2 : 2], identity[:])
-            grouped = sb.tile([P, P, PACK], BF16, name="xt%d_grouped" % t, align_bytes=64)
+            grouped = xg[t // 2][:, (t % 2) * P : (t % 2 + 1) * P, :]
             copy(
                 engine,
-                grouped[:].rearrange("p w t -> p (w t)").bitcast(F32).rearrange("p (w u) -> p w u", u=2),
+                grouped.rearrange("p w t -> p (w t)").bitcast(F32).rearrange("p (w u) -> p w u", u=2),
                 turned[:].rearrange("p u w -> p w u"),
             )
-            return grouped
 
         def stage1(first_bank, q, c0, dst, d0, name, engine):
             acc = bank(first_bank, [P, PACK, P], name)
             for t in range(PACK):
-                mm(acc[:, t, :], xq[t], 0, q, c0, P, True, True)
+                mm(acc[:, t, :], xq[t // 2], (t % 2) * P, q, c0, P, True, True)
             copy(engine, dst[:, d0 : d0 + P, :], acc[:].rearrange("p t j -> p j t"))
 
-        for t in range(PACK - 1):
-            quantise(xq[t], 0, tokens(t, "s"))
-        last_tokens = tokens(PACK - 1, "s")
+        for t in range(PACK):
+            tokens(t, "s")
+            if t == 2:
+                quantise(xq[0], 0, xg[0])
 
         ciq = [mx_tiles(H, "ciq%d" % h) for h in range(2)]
         siq = [mx_tiles(H, "siq%d" % h) for h in range(2)]
         ceq = [mx_tiles(H, "ceq%d" % h) for h in range(2)]
-        seq = [mx_tiles(H, "seq%d" % h) for h in range(2)]
-        aq = mx_tiles(J, "aq")
-        bq = mx_tiles(J, "bq")
-        ag = [sb.tile([P, H, PACK], BF16, name="ag%d" % h, align_bytes=64) for h in range(2)]
+        seq0 = mx_tiles(H, "seq0")
+        seq2 = mx_tiles(P, "seq2")
+        seq3 = mx_tiles(P, "seq3")
+        aq = [mx_tiles(H, "aq%d" % h) for h in range(2)]
+        bq = [mx_tiles(H, "bq%d" % h) for h in range(2)]
         bg = [sb.tile([P, H, PACK], BF16, name="bg%d" % h, align_bytes=64) for h in range(2)]
 
+        def weave2(raw, name):
+            grouped = sb.tile([P, H, PACK], BF16, name=name + "_grouped", tag=name + "_grouped", align_bytes=64)
+            for engine, c0 in (("s", P), ("v", 0)):
+                copy(
+                    engine,
+                    grouped[:, c0 : c0 + P, :].rearrange("p (c i) t -> p c t i", i=LINE),
+                    raw[:, :, c0 : c0 + P].rearrange("p t (c i) -> p c t i", i=LINE),
+                )
+            return grouped
+
         def half_stage1(first_bank, q, dst, name):
+            accs = [bank(first_bank + c, [P, PACK, P], "%s%d" % (name, c)) for c in range(2)]
+            for g in range(2):
+                for c in range(2):
+                    for t in (2 * g, 2 * g + 1):
+                        mm(accs[c][:, t, :], xq[g], (t % 2) * P, q, c * P, P, True, True)
+                    if g == 1:
+                        copy("s", dst[:, c * P : (c + 1) * P, :], accs[c][:].rearrange("p t j -> p j t"))
+
+        def whole_stage1(first_bank, q, dst, name):
             for c in range(2):
                 stage1(first_bank + c, q, c * P, dst, c * P, "%s%d" % (name, c), "s")
 
-        def finish(c, parts):
-            result = sb.tile([P, J], F32, name="result%d" % c)
-            for n, engine, j0, width in parts:
-                acc = bank(n, [P, width], "y%d_%d" % (c, j0))
-                mm(acc[:], ceq[c // 2], (c % 2) * P, aq, j0, width, True, False)
-                mm(acc[:], seq[c // 2], (c % 2) * P, bq, j0, width, False, True)
-                copy(engine, result[:, j0 : j0 + width], acc[:])
-            nc.sync.dma_start(out=out[c * P : (c + 1) * P, :], in_=result[:])
+        def begin(c, h):
+            acc = bank((0, 1, 4, 6)[c] + (2, 2, 1, 1)[c] * h, [P, H], "y%d_%d" % (c, h))
+            mm(acc[:], ceq[c // 2], (c % 2) * P, aq[h], 0, H, True, False)
+            return acc
 
-        ci0 = weave("v", ci_raw[0], 0, H, "ci0")
-        quantise(xq[PACK - 1], 0, last_tokens)
+        def finish(acc, sq, s0, c, h, engine, result=None):
+            mm(acc[:], sq, s0, bq[h], 0, H, False, True)
+            if result is None:
+                result = sb.tile([P, H], F32, name="result%d_%d" % (c, h))[:]
+            copy(engine, result, acc[:])
+            nc.sync.dma_start(out=out[c * P : (c + 1) * P, h * H : (h + 1) * H], in_=result)
+
+        def clock(src, name):
+            tick = sb.tile([P, 1], src.dtype, name=name)
+            nc.gpsimd.tensor_copy(out=tick[:], in_=src)
+
+        ci0 = weave("v", ci0_raw, 0, H, "ci0")
         quantise(ciq[0], 0, ci0)
-        ci1 = weave("s", ci_raw[1], 0, H, "ci1")
-        half_stage1(0, ciq[0], ag[0], "a0")
-        si0 = weave("v", si_raw[0], 0, H, "si0")
-        quantise(ciq[1], 0, ci1)
+        xq.append(mx_tiles(2 * P, "xq1", tag="ci0_grouped"))
+        quantise(xq[1], 0, xg[1])
+        si0 = weave("s", si0_raw, 0, H, "si0")
         quantise(siq[0], 0, si0)
-        half_stage1(2, ciq[1], ag[1], "a1")
-        half_stage1(4, siq[0], bg[0], "b0")
-        si1 = weave("v", si_raw[1], 0, H, "si1")
-        quantise(aq, 0, ag[0])
+        ci1 = weave2(ci1_raw, "ci1")
+        ag = [
+            sb.tile([P, H, PACK], BF16, name="ag0", tag="ci1_raw", align_bytes=64),
+            sb.tile([P, H, PACK], BF16, name="ag1", align_bytes=64),
+        ]
+        half_stage1(0, ciq[0], ag[0], "a0")
+        quantise(ciq[1], 0, ci1)
+        whole_stage1(2, siq[0], bg[0], "b0")
+        whole_stage1(4, ciq[1], ag[1], "a1")
+        si1 = weave("v", si1_raw, 0, H, "si1")
+        quantise(aq[0], 0, ag[0])
         quantise(siq[1], 0, si1)
-        half_stage1(6, siq[1], bg[1], "b1")
+        whole_stage1(6, siq[1], bg[1], "b1")
         ce0 = weave("v", ce0_raw, 0, H, "ce0")
-        quantise(aq, H, ag[1])
+        quantise(bq[0], 0, bg[0])
         quantise(ceq[0], 0, ce0)
         se0 = weave("v", se0_raw, 0, H, "se0")
-        quantise(bq, 0, bg[0])
-        quantise(seq[0], 0, se0)
-        ce1 = weave("s", ce1_raw, 0, H, "ce1")
-        quantise(bq, H, bg[1])
-        finish(0, [(0, "s", 0, J)])
-        se1 = weave("v", se1_raw, 0, H, "se1")
+        quantise(aq[1], 0, ag[1])
+        quantise(seq0, 0, se0)
+        ce1 = weave2(ce1_raw, "ce1")
+        quantise(bq[1], 0, bg[1])
         quantise(ceq[1], 0, ce1)
-        quantise(seq[1], 0, se1)
-        finish(1, [(1, "s", 0, J)])
-        finish(2, [(2, "v", 0, J)])
-        finish(3, [(4, "s", 0, H), (5, "v", H, H)])
+        accs = [[begin(c, h) for h in range(2)] for c in range(4)]
+        ahead = sb.tile([P, 2, H], F32, name="ahead", tag="ce1_raw", align_bytes=64)
+        for c in range(2):
+            finish(accs[c][0], seq0, c * P, c, 0, "s", ahead[:, c, :])
+        se2 = weave("v", se1_raw, 0, P, "se2")
+        se3 = weave("s", se1_raw, P, P, "se3")
+        behind = sb.tile([P, 2, H], F32, name="behind", tag="se1_raw", align_bytes=64)
+        for c in range(2):
+            finish(accs[c][1], seq0, c * P, c, 1, "s", behind[:, c, :])
+        quantise(seq2, 0, se2)
+        quantise(seq3, 0, se3)
+        for c, sq in ((2, seq2), (3, seq3)):
+            for h in range(2):
+                finish(accs[c][h], sq, 0, c, h, "sv"[h])

@@ -15,198 +15,200 @@ FP8X4 = mybir.dt.float8_e4m3fn_x4
 
 P = 128
 PACK = 4
-LINE = 2
+HALF = 256
+WALK = 2
+GROUP = 16
+ALIGN = 64
 
 
 def tile_attend_fouriermix_kernel(tc, tok, ci, si, ce, se, offs, out):
     nc = tc.nc
+    vector_copy, scalar_copy = nc.vector.tensor_copy, nc.scalar.copy
+
     with ExitStack() as ctx:
         sb = ctx.enter_context(tc.tile_pool(name="sb", bufs=1))
         ps = ctx.enter_context(tc.psum_pool(name="ps", bufs=1))
 
+        def sbuf(shape, dtype, name, over=None):
+            return sb.tile(shape, dtype, name=name, tag=over or name, align_bytes=ALIGN)
+
         def bank(n, shape, name):
             return ps.tile(shape, F32, name=name, tag="bank%d" % n)
 
-        def mx_tiles(width, name, tag=None):
-            codes = sb.tile([P, width], U32, name=name + "_codes", tag=tag or name + "_codes", align_bytes=64)
-            scales = sb.tile([P, width], U8, name=name + "_scales", align_bytes=64)
-            return codes, scales
+        def mx_operand(width, name, over=None):
+            return sbuf([P, width], U32, name + "_codes", over), sbuf([P, width], U8, name + "_scales")
 
-        def quantise(dst, c0, grouped):
-            width = grouped.shape[1]
+        def quantise(operand, woven):
+            codes, scales = operand
             nc.vector.quantize_mx(
-                out=dst[0][:, c0 : c0 + width].bitcast(FP8X4),
-                scales=dst[1][:, c0 : c0 + width],
-                in_=grouped[:].rearrange("p w t -> p (w t)"),
+                out=codes[:].bitcast(FP8X4),
+                scales=scales[:],
+                in_=woven[:].rearrange("p c t -> p (c t)"),
             )
 
-        def copy(engine, dst, src):
-            if engine == "v":
-                nc.vector.tensor_copy(out=dst, in_=src)
-            else:
-                nc.scalar.copy(out=dst, in_=src)
-
-        def load(matrix, c0, width, name):
-            raw = sb.tile([P, PACK, width], F32, name=name + "_raw", tag=name + "_raw", align_bytes=64)
-            nc.sync.dma_start(out=raw[:], in_=matrix[:, c0 : c0 + width].rearrange("(p t) w -> p t w", t=PACK))
-            return raw
-
-        def weave(engine, raw, c0, width, name):
-            grouped = sb.tile([P, width, PACK], BF16, name=name + "_grouped", tag=name + "_grouped", align_bytes=64)
-            copy(
-                engine,
-                grouped[:].rearrange("p (c i) t -> p c t i", i=LINE),
-                raw[:, :, c0 : c0 + width].rearrange("p t (c i) -> p c t i", i=LINE),
-            )
-            return grouped
-
-        def mm(dst, lhs, l0, rhs, r0, n, start, stop):
+        def product(dst, lhs, lhs_col, rhs, rhs_col, n, start, stop):
             nc.tensor.matmul_mx(
                 out=dst,
-                lhsT=lhs[0][:, l0 : l0 + P].bitcast(FP8X4),
-                lhsT_scale=lhs[1][:, l0 : l0 + P],
-                rhs=rhs[0][:, r0 : r0 + n].bitcast(FP8X4),
-                rhs_scale=rhs[1][:, r0 : r0 + n],
+                lhsT=lhs[0][:, lhs_col : lhs_col + P].bitcast(FP8X4),
+                lhsT_scale=lhs[1][:, lhs_col : lhs_col + P],
+                rhs=rhs[0][:, rhs_col : rhs_col + n].bitcast(FP8X4),
+                rhs_scale=rhs[1][:, rhs_col : rhs_col + n],
                 start=start,
                 stop=stop,
             )
 
+        def load_half(matrix, h, name):
+            raw = sbuf([P, PACK, HALF], F32, name + "_raw")
+            columns = matrix[:, h * HALF : (h + 1) * HALF]
+            nc.sync.dma_start(out=raw[:], in_=columns.rearrange("(p t) c -> p t c", t=PACK))
+            return raw
+
+        def weave_columns(copy, dst, src):
+            copy(
+                out=dst.rearrange("p (c i) t -> p c t i", i=WALK),
+                in_=src.rearrange("p t (c i) -> p c t i", i=WALK),
+            )
+
+        def weave(copy, raw, first, width, name):
+            woven = sbuf([P, width, PACK], BF16, name + "_woven")
+            weave_columns(copy, woven[:], raw[:, :, first : first + width])
+            return woven
+
+        def weave_shared(raw, name):
+            woven = sbuf([P, HALF, PACK], BF16, name + "_woven")
+            weave_columns(scalar_copy, woven[:, P:HALF, :], raw[:, :, P:HALF])
+            weave_columns(vector_copy, woven[:, 0:P, :], raw[:, :, 0:P])
+            return woven
+
         identity = sb.tile([P, P], F32, name="identity")
         make_identity(nc, identity[:])
 
-        offsets = sb.tile([P, I // 16], U16, name="offsets")
+        offsets = sb.tile([P, I // GROUP], U16, name="offsets")
         planes = [sb.tile([P, T], F32, name="plane%d" % t) for t in range(PACK)]
         tok_planes = tok.rearrange("(p t) n -> t p n", t=PACK)
         nc.sync.dma_start(out=planes[0][:], in_=tok_planes[0])
         nc.sync.dma_start(offsets[:], offs)
         for t in range(1, PACK):
             nc.sync.dma_start(out=planes[t][:], in_=tok_planes[t])
-        H = 256
-        ci0_raw = load(ci, 0, H, "ci0")
-        si0_raw = load(si, 0, H, "si0")
-        ci1_raw = load(ci, H, H, "ci1")
-        si1_raw = load(si, H, H, "si1")
-        ce0_raw = load(ce, 0, H, "ce0")
-        se0_raw = load(se, 0, H, "se0")
-        ce1_raw = load(ce, H, H, "ce1")
-        se1_raw = load(se, H, H, "se1")
+        ci0_raw = load_half(ci, 0, "ci0")
+        si0_raw = load_half(si, 0, "si0")
+        ci1_raw = load_half(ci, 1, "ci1")
+        si1_raw = load_half(si, 1, "si1")
+        ce0_raw = load_half(ce, 0, "ce0")
+        se0_raw = load_half(se, 0, "se0")
+        ce1_raw = load_half(ce, 1, "ce1")
+        se1_raw = load_half(se, 1, "se1")
 
-        xq = [mx_tiles(2 * P, "xq0")]
-        xg = [sb.tile([P, 2 * P, PACK], BF16, name="xg%d" % g, align_bytes=64) for g in range(2)]
-
-        def tokens(t, engine):
-            picked = sb.tile([P, I], BF16, name="picked%d" % t, align_bytes=64)
+        def gather_and_turn(t):
+            picked = sbuf([P, I], BF16, "picked%d" % t)
             nc.vector.tensor_copy(picked[:], planes[t][:].indirect(offsets[:]))
-            words = picked[:].bitcast(F32)
-            turned = bank(4 + t, [P, 2, P], "turned%d" % t)
+            pairs = picked[:].bitcast(F32)
+            turned = bank(PACK + t, [P, 2, P], "turned%d" % t)
             for u in range(2):
-                nc.tensor.transpose(turned[:, u, :], words[:, u : I // 2 : 2], identity[:])
-            grouped = xg[t // 2][:, (t % 2) * P : (t % 2 + 1) * P, :]
+                nc.tensor.transpose(turned[:, u, :], pairs[:, u : I // 2 : 2], identity[:])
+            return turned
+
+        def weave_turned(copy, woven, t, turned):
+            columns = woven[:, (t % 2) * P : (t % 2 + 1) * P, :]
             copy(
-                engine,
-                grouped.rearrange("p w t -> p (w t)").bitcast(F32).rearrange("p (w u) -> p w u", u=2),
-                turned[:].rearrange("p u w -> p w u"),
+                out=columns.rearrange("p c t -> p (c t)").bitcast(F32).rearrange("p (c u) -> p c u", u=2),
+                in_=turned[:].rearrange("p u c -> p c u"),
             )
 
-        def stage1(first_bank, q, c0, dst, d0, name, engine):
-            acc = bank(first_bank, [P, PACK, P], name)
-            for t in range(PACK):
-                mm(acc[:, t, :], xq[t // 2], (t % 2) * P, q, c0, P, True, True)
-            copy(engine, dst[:, d0 : d0 + P, :], acc[:].rearrange("p t j -> p j t"))
+        xq = [mx_operand(2 * P, "xq0")]
+        xt0 = sbuf([P, 2 * P, PACK], BF16, "xt0_woven")
+        for t in range(2):
+            weave_turned(scalar_copy, xt0, t, gather_and_turn(t))
+        turned2 = gather_and_turn(2)
+        quantise(xq[0], xt0)
+        turned3 = gather_and_turn(3)
 
-        for t in range(PACK):
-            tokens(t, "s")
-            if t == 2:
-                quantise(xq[0], 0, xg[0])
+        ciq = [mx_operand(HALF, "ciq%d" % h) for h in range(2)]
+        siq = [mx_operand(HALF, "siq%d" % h) for h in range(2)]
+        ceq = [mx_operand(HALF, "ceq%d" % h) for h in range(2)]
+        seq0 = mx_operand(HALF, "seq0")
+        seq2 = mx_operand(P, "seq2")
+        seq3 = mx_operand(P, "seq3")
+        aq = [mx_operand(HALF, "aq%d" % h) for h in range(2)]
+        bq = [mx_operand(HALF, "bq%d" % h) for h in range(2)]
+        bt = [sbuf([P, HALF, PACK], BF16, "bt%d_woven" % h) for h in range(2)]
 
-        ciq = [mx_tiles(H, "ciq%d" % h) for h in range(2)]
-        siq = [mx_tiles(H, "siq%d" % h) for h in range(2)]
-        ceq = [mx_tiles(H, "ceq%d" % h) for h in range(2)]
-        seq0 = mx_tiles(H, "seq0")
-        seq2 = mx_tiles(P, "seq2")
-        seq3 = mx_tiles(P, "seq3")
-        aq = [mx_tiles(H, "aq%d" % h) for h in range(2)]
-        bq = [mx_tiles(H, "bq%d" % h) for h in range(2)]
-        bg = [sb.tile([P, H, PACK], BF16, name="bg%d" % h, align_bytes=64) for h in range(2)]
+        def slot_product(acc, t, rhs, c):
+            product(acc[:, t, :], xq[t // 2], (t % 2) * P, rhs, c * P, P, True, True)
 
-        def weave2(raw, name):
-            grouped = sb.tile([P, H, PACK], BF16, name=name + "_grouped", tag=name + "_grouped", align_bytes=64)
-            for engine, c0 in (("s", P), ("v", 0)):
-                copy(
-                    engine,
-                    grouped[:, c0 : c0 + P, :].rearrange("p (c i) t -> p c t i", i=LINE),
-                    raw[:, :, c0 : c0 + P].rearrange("p t (c i) -> p c t i", i=LINE),
-                )
-            return grouped
+        def weave_bank(woven, c, acc):
+            scalar_copy(out=woven[:, c * P : (c + 1) * P, :], in_=acc[:].rearrange("p t j -> p j t"))
 
-        def half_stage1(first_bank, q, dst, name):
-            accs = [bank(first_bank + c, [P, PACK, P], "%s%d" % (name, c)) for c in range(2)]
-            for g in range(2):
-                for c in range(2):
-                    for t in (2 * g, 2 * g + 1):
-                        mm(accs[c][:, t, :], xq[g], (t % 2) * P, q, c * P, P, True, True)
-                    if g == 1:
-                        copy("s", dst[:, c * P : (c + 1) * P, :], accs[c][:].rearrange("p t j -> p j t"))
-
-        def whole_stage1(first_bank, q, dst, name):
+        def over_slots(first_bank, rhs, woven, name):
             for c in range(2):
-                stage1(first_bank + c, q, c * P, dst, c * P, "%s%d" % (name, c), "s")
+                acc = bank(first_bank + c, [P, PACK, P], "%s%d" % (name, c))
+                for t in range(PACK):
+                    slot_product(acc, t, rhs, c)
+                weave_bank(woven, c, acc)
 
-        def begin(c, h):
-            acc = bank((0, 1, 4, 6)[c] + (2, 2, 1, 1)[c] * h, [P, H], "y%d_%d" % (c, h))
-            mm(acc[:], ceq[c // 2], (c % 2) * P, aq[h], 0, H, True, False)
+        def over_slots_first(rhs, woven, name):
+            accs = [bank(c, [P, PACK, P], "%s%d" % (name, c)) for c in range(2)]
+            for c in range(2):
+                for t in (0, 1):
+                    slot_product(accs[c], t, rhs, c)
+            for c in range(2):
+                for t in (2, 3):
+                    slot_product(accs[c], t, rhs, c)
+                weave_bank(woven, c, accs[c])
+
+        def open_block(c, h):
+            n = c + 2 * h if c < 2 else 2 * c + h
+            acc = bank(n, [P, HALF], "block%d_%d" % (c, h))
+            product(acc[:], ceq[c // 2], (c % 2) * P, aq[h], 0, HALF, True, False)
             return acc
 
-        def finish(acc, sq, s0, c, h, engine, result=None):
-            mm(acc[:], sq, s0, bq[h], 0, H, False, True)
-            if result is None:
-                result = sb.tile([P, H], F32, name="result%d_%d" % (c, h))[:]
-            copy(engine, result, acc[:])
-            nc.sync.dma_start(out=out[c * P : (c + 1) * P, h * H : (h + 1) * H], in_=result)
+        def close_block(c, h, se_operand, se_col, copy, result):
+            acc = blocks[c][h]
+            product(acc[:], se_operand, se_col, bq[h], 0, HALF, False, True)
+            copy(out=result, in_=acc[:])
+            nc.sync.dma_start(out=out[c * P : (c + 1) * P, h * HALF : (h + 1) * HALF], in_=result)
 
-        def clock(src, name):
-            tick = sb.tile([P, 1], src.dtype, name=name)
-            nc.gpsimd.tensor_copy(out=tick[:], in_=src)
+        ci0 = weave(vector_copy, ci0_raw, 0, HALF, "ci0")
+        xt1 = sbuf([P, 2 * P, PACK], BF16, "xt1_woven", over="ci0_raw")
+        weave_turned(scalar_copy, xt1, 2, turned2)
+        weave_turned(vector_copy, xt1, 3, turned3)
+        quantise(ciq[0], ci0)
+        xq.append(mx_operand(2 * P, "xq1", over="ci0_woven"))
+        quantise(xq[1], xt1)
+        si0 = weave(scalar_copy, si0_raw, 0, HALF, "si0")
+        quantise(siq[0], si0)
+        ci1 = weave_shared(ci1_raw, "ci1")
+        at = [sbuf([P, HALF, PACK], BF16, "at0_woven", over="ci1_raw"), sbuf([P, HALF, PACK], BF16, "at1_woven")]
+        over_slots_first(ciq[0], at[0], "a0")
+        quantise(ciq[1], ci1)
+        over_slots(2, siq[0], bt[0], "b0")
+        over_slots(4, ciq[1], at[1], "a1")
+        si1 = weave(vector_copy, si1_raw, 0, HALF, "si1")
+        quantise(aq[0], at[0])
+        quantise(siq[1], si1)
+        over_slots(6, siq[1], bt[1], "b1")
+        ce0 = weave(vector_copy, ce0_raw, 0, HALF, "ce0")
+        quantise(bq[0], bt[0])
+        quantise(ceq[0], ce0)
+        se0 = weave(vector_copy, se0_raw, 0, HALF, "se0")
+        quantise(aq[1], at[1])
+        quantise(seq0, se0)
+        ce1 = weave_shared(ce1_raw, "ce1")
+        quantise(bq[1], bt[1])
+        quantise(ceq[1], ce1)
 
-        ci0 = weave("v", ci0_raw, 0, H, "ci0")
-        quantise(ciq[0], 0, ci0)
-        xq.append(mx_tiles(2 * P, "xq1", tag="ci0_grouped"))
-        quantise(xq[1], 0, xg[1])
-        si0 = weave("s", si0_raw, 0, H, "si0")
-        quantise(siq[0], 0, si0)
-        ci1 = weave2(ci1_raw, "ci1")
-        ag = [
-            sb.tile([P, H, PACK], BF16, name="ag0", tag="ci1_raw", align_bytes=64),
-            sb.tile([P, H, PACK], BF16, name="ag1", align_bytes=64),
-        ]
-        half_stage1(0, ciq[0], ag[0], "a0")
-        quantise(ciq[1], 0, ci1)
-        whole_stage1(2, siq[0], bg[0], "b0")
-        whole_stage1(4, ciq[1], ag[1], "a1")
-        si1 = weave("v", si1_raw, 0, H, "si1")
-        quantise(aq[0], 0, ag[0])
-        quantise(siq[1], 0, si1)
-        whole_stage1(6, siq[1], bg[1], "b1")
-        ce0 = weave("v", ce0_raw, 0, H, "ce0")
-        quantise(bq[0], 0, bg[0])
-        quantise(ceq[0], 0, ce0)
-        se0 = weave("v", se0_raw, 0, H, "se0")
-        quantise(aq[1], 0, ag[1])
-        quantise(seq0, 0, se0)
-        ce1 = weave2(ce1_raw, "ce1")
-        quantise(bq[1], 0, bg[1])
-        quantise(ceq[1], 0, ce1)
-        accs = [[begin(c, h) for h in range(2)] for c in range(4)]
-        ahead = sb.tile([P, 2, H], F32, name="ahead", tag="ce1_raw", align_bytes=64)
+        blocks = [[open_block(c, h) for h in range(2)] for c in range(PACK)]
+        upper_left = sbuf([P, 2, HALF], F32, "upper_left", over="ce1_raw")
         for c in range(2):
-            finish(accs[c][0], seq0, c * P, c, 0, "s", ahead[:, c, :])
-        se2 = weave("v", se1_raw, 0, P, "se2")
-        se3 = weave("s", se1_raw, P, P, "se3")
-        behind = sb.tile([P, 2, H], F32, name="behind", tag="se1_raw", align_bytes=64)
+            close_block(c, 0, seq0, c * P, scalar_copy, upper_left[:, c, :])
+        se2 = weave(vector_copy, se1_raw, 0, P, "se2")
+        se3 = weave(scalar_copy, se1_raw, P, P, "se3")
+        upper_right = sbuf([P, 2, HALF], F32, "upper_right", over="se1_raw")
         for c in range(2):
-            finish(accs[c][1], seq0, c * P, c, 1, "s", behind[:, c, :])
-        quantise(seq2, 0, se2)
-        quantise(seq3, 0, se3)
-        for c, sq in ((2, seq2), (3, seq3)):
-            for h in range(2):
-                finish(accs[c][h], sq, 0, c, h, "sv"[h])
+            close_block(c, 1, seq0, c * P, scalar_copy, upper_right[:, c, :])
+        quantise(seq2, se2)
+        quantise(seq3, se3)
+        for c, se_operand in ((2, seq2), (3, seq3)):
+            for h, copy in ((0, scalar_copy), (1, vector_copy)):
+                result = sb.tile([P, HALF], F32, name="result%d_%d" % (c, h))
+                close_block(c, h, se_operand, 0, copy, result[:])

from contextlib import ExitStack

import concourse.mybir as mybir
from concourse.masks import make_identity

E, T, I, J, F = 512, 2048, 512, 512, 512
FLOPS = 2 * (2 * I * J * E + 2 * E * F * J)

F32 = mybir.dt.float32
BF16 = mybir.dt.bfloat16
U32 = mybir.dt.uint32
U16 = mybir.dt.uint16
U8 = mybir.dt.uint8
FP8X4 = mybir.dt.float8_e4m3fn_x4

P = 128
PACK = 4
HALF = 256
WALK = 2
GROUP = 16
ALIGN = 64


def tile_attend_fouriermix_kernel(tc, tok, ci, si, ce, se, offs, out):
    nc = tc.nc
    vector_copy, scalar_copy = nc.vector.tensor_copy, nc.scalar.copy

    with ExitStack() as ctx:
        sb = ctx.enter_context(tc.tile_pool(name="sb", bufs=1))
        ps = ctx.enter_context(tc.psum_pool(name="ps", bufs=1))

        def sbuf(shape, dtype, name, over=None):
            return sb.tile(shape, dtype, name=name, tag=over or name, align_bytes=ALIGN)

        def bank(n, shape, name):
            return ps.tile(shape, F32, name=name, tag="bank%d" % n)

        def mx_operand(width, name, over=None):
            return sbuf([P, width], U32, name + "_codes", over), sbuf([P, width], U8, name + "_scales")

        def quantise(operand, woven):
            codes, scales = operand
            nc.vector.quantize_mx(
                out=codes[:].bitcast(FP8X4),
                scales=scales[:],
                in_=woven[:].rearrange("p c t -> p (c t)"),
            )

        def product(dst, lhs, lhs_col, rhs, rhs_col, n, start, stop):
            nc.tensor.matmul_mx(
                out=dst,
                lhsT=lhs[0][:, lhs_col : lhs_col + P].bitcast(FP8X4),
                lhsT_scale=lhs[1][:, lhs_col : lhs_col + P],
                rhs=rhs[0][:, rhs_col : rhs_col + n].bitcast(FP8X4),
                rhs_scale=rhs[1][:, rhs_col : rhs_col + n],
                start=start,
                stop=stop,
            )

        def load_half(matrix, h, name):
            raw = sbuf([P, PACK, HALF], F32, name + "_raw")
            columns = matrix[:, h * HALF : (h + 1) * HALF]
            nc.sync.dma_start(out=raw[:], in_=columns.rearrange("(p t) c -> p t c", t=PACK))
            return raw

        def weave_columns(copy, dst, src):
            copy(
                out=dst.rearrange("p (c i) t -> p c t i", i=WALK),
                in_=src.rearrange("p t (c i) -> p c t i", i=WALK),
            )

        def weave(copy, raw, first, width, name):
            woven = sbuf([P, width, PACK], BF16, name + "_woven")
            weave_columns(copy, woven[:], raw[:, :, first : first + width])
            return woven

        def weave_shared(raw, name):
            woven = sbuf([P, HALF, PACK], BF16, name + "_woven")
            weave_columns(scalar_copy, woven[:, P:HALF, :], raw[:, :, P:HALF])
            weave_columns(vector_copy, woven[:, 0:P, :], raw[:, :, 0:P])
            return woven

        identity = sb.tile([P, P], F32, name="identity")
        make_identity(nc, identity[:])

        offsets = sb.tile([P, I // GROUP], U16, name="offsets")
        planes = [sb.tile([P, T], F32, name="plane%d" % t) for t in range(PACK)]
        tok_planes = tok.rearrange("(p t) n -> t p n", t=PACK)
        nc.sync.dma_start(out=planes[0][:], in_=tok_planes[0])
        nc.sync.dma_start(offsets[:], offs)
        for t in range(1, PACK):
            nc.sync.dma_start(out=planes[t][:], in_=tok_planes[t])
        ci0_raw = load_half(ci, 0, "ci0")
        si0_raw = load_half(si, 0, "si0")
        ci1_raw = load_half(ci, 1, "ci1")
        si1_raw = load_half(si, 1, "si1")
        ce0_raw = load_half(ce, 0, "ce0")
        se0_raw = load_half(se, 0, "se0")
        ce1_raw = load_half(ce, 1, "ce1")
        se1_raw = load_half(se, 1, "se1")

        def gather_and_turn(t):
            picked = sbuf([P, I], BF16, "picked%d" % t)
            nc.vector.tensor_copy(picked[:], planes[t][:].indirect(offsets[:]))
            pairs = picked[:].bitcast(F32)
            turned = bank(PACK + t, [P, 2, P], "turned%d" % t)
            for u in range(2):
                nc.tensor.transpose(turned[:, u, :], pairs[:, u : I // 2 : 2], identity[:])
            return turned

        def weave_turned(copy, woven, t, turned):
            columns = woven[:, (t % 2) * P : (t % 2 + 1) * P, :]
            copy(
                out=columns.rearrange("p c t -> p (c t)").bitcast(F32).rearrange("p (c u) -> p c u", u=2),
                in_=turned[:].rearrange("p u c -> p c u"),
            )

        xq = [mx_operand(2 * P, "xq0")]
        xt0 = sbuf([P, 2 * P, PACK], BF16, "xt0_woven")
        for t in range(2):
            weave_turned(scalar_copy, xt0, t, gather_and_turn(t))
        turned2 = gather_and_turn(2)
        quantise(xq[0], xt0)
        turned3 = gather_and_turn(3)

        ciq = [mx_operand(HALF, "ciq%d" % h) for h in range(2)]
        siq = [mx_operand(HALF, "siq%d" % h) for h in range(2)]
        ceq = [mx_operand(HALF, "ceq%d" % h) for h in range(2)]
        seq0 = mx_operand(HALF, "seq0")
        seq2 = mx_operand(P, "seq2")
        seq3 = mx_operand(P, "seq3")
        aq = [mx_operand(HALF, "aq%d" % h) for h in range(2)]
        bq = [mx_operand(HALF, "bq%d" % h) for h in range(2)]
        bt = [sbuf([P, HALF, PACK], BF16, "bt%d_woven" % h) for h in range(2)]

        def slot_product(acc, t, rhs, c):
            product(acc[:, t, :], xq[t // 2], (t % 2) * P, rhs, c * P, P, True, True)

        def weave_bank(woven, c, acc):
            scalar_copy(out=woven[:, c * P : (c + 1) * P, :], in_=acc[:].rearrange("p t j -> p j t"))

        def over_slots(first_bank, rhs, woven, name):
            for c in range(2):
                acc = bank(first_bank + c, [P, PACK, P], "%s%d" % (name, c))
                for t in range(PACK):
                    slot_product(acc, t, rhs, c)
                weave_bank(woven, c, acc)

        def over_slots_first(rhs, woven, name):
            accs = [bank(c, [P, PACK, P], "%s%d" % (name, c)) for c in range(2)]
            for c in range(2):
                for t in (0, 1):
                    slot_product(accs[c], t, rhs, c)
            for c in range(2):
                for t in (2, 3):
                    slot_product(accs[c], t, rhs, c)
                weave_bank(woven, c, accs[c])

        def open_block(c, h):
            n = c + 2 * h if c < 2 else 2 * c + h
            acc = bank(n, [P, HALF], "block%d_%d" % (c, h))
            product(acc[:], ceq[c // 2], (c % 2) * P, aq[h], 0, HALF, True, False)
            return acc

        def close_block(c, h, se_operand, se_col, copy, result):
            acc = blocks[c][h]
            product(acc[:], se_operand, se_col, bq[h], 0, HALF, False, True)
            copy(out=result, in_=acc[:])
            nc.sync.dma_start(out=out[c * P : (c + 1) * P, h * HALF : (h + 1) * HALF], in_=result)

        ci0 = weave(vector_copy, ci0_raw, 0, HALF, "ci0")
        xt1 = sbuf([P, 2 * P, PACK], BF16, "xt1_woven", over="ci0_raw")
        weave_turned(scalar_copy, xt1, 2, turned2)
        weave_turned(vector_copy, xt1, 3, turned3)
        quantise(ciq[0], ci0)
        xq.append(mx_operand(2 * P, "xq1", over="ci0_woven"))
        quantise(xq[1], xt1)
        si0 = weave(scalar_copy, si0_raw, 0, HALF, "si0")
        quantise(siq[0], si0)
        ci1 = weave_shared(ci1_raw, "ci1")
        at = [sbuf([P, HALF, PACK], BF16, "at0_woven", over="ci1_raw"), sbuf([P, HALF, PACK], BF16, "at1_woven")]
        over_slots_first(ciq[0], at[0], "a0")
        quantise(ciq[1], ci1)
        over_slots(2, siq[0], bt[0], "b0")
        over_slots(4, ciq[1], at[1], "a1")
        si1 = weave(vector_copy, si1_raw, 0, HALF, "si1")
        quantise(aq[0], at[0])
        quantise(siq[1], si1)
        over_slots(6, siq[1], bt[1], "b1")
        ce0 = weave(vector_copy, ce0_raw, 0, HALF, "ce0")
        quantise(bq[0], bt[0])
        quantise(ceq[0], ce0)
        se0 = weave(vector_copy, se0_raw, 0, HALF, "se0")
        quantise(aq[1], at[1])
        quantise(seq0, se0)
        ce1 = weave_shared(ce1_raw, "ce1")
        quantise(bq[1], bt[1])
        quantise(ceq[1], ce1)

        blocks = [[open_block(c, h) for h in range(2)] for c in range(PACK)]
        upper_left = sbuf([P, 2, HALF], F32, "upper_left", over="ce1_raw")
        for c in range(2):
            close_block(c, 0, seq0, c * P, scalar_copy, upper_left[:, c, :])
        se2 = weave(vector_copy, se1_raw, 0, P, "se2")
        se3 = weave(scalar_copy, se1_raw, P, P, "se3")
        upper_right = sbuf([P, 2, HALF], F32, "upper_right", over="se1_raw")
        for c in range(2):
            close_block(c, 1, seq0, c * P, scalar_copy, upper_right[:, c, :])
        quantise(seq2, se2)
        quantise(seq3, se3)
        for c, se_operand in ((2, seq2), (3, seq3)):
            for h, copy in ((0, scalar_copy), (1, vector_copy)):
                result = sb.tile([P, HALF], F32, name="result%d_%d" % (c, h))
                close_block(c, h, se_operand, 0, copy, result[:])
